import numpy as np
import ml_dtypes


def mxq(x, axis, fmt="e4m3"):
    dtype, down = {"e4m3": (ml_dtypes.float8_e4m3fn, 7), "e5m2": (ml_dtypes.float8_e5m2, 14)}[fmt]
    v = np.moveaxis(np.asarray(x, np.float32).astype(ml_dtypes.bfloat16).astype(np.float64), axis, -1)
    blocks = v.reshape(v.shape[:-1] + (-1, 32))
    amax = np.abs(blocks).max(-1, keepdims=True)
    byte = np.maximum(np.where(amax > 0, np.frexp(amax)[1] - 1 + 127, 0) - down, 1)
    scale = np.exp2(byte - 127.0)
    codes = (blocks / scale).astype(np.float32).astype(dtype).astype(np.float64)
    return np.moveaxis((codes * scale).reshape(v.shape), -1, axis)


WIDE = False


def mx_kscale(k):
    if not WIDE:
        return np.ones(k)
    levels = np.array([10, -10, 5, -5, 0])
    if k % 512:
        return np.exp2(np.random.permutation(np.resize(levels, k // 32))).repeat(32)
    a = np.empty((k // 512, 16))
    for p in range(k // 512):
        a[p, :8] = np.random.permutation(np.resize(levels, 8))
        for g in range(8):
            far = levels[np.abs(levels - a[p, g]) >= 10]
            a[p, g + 8] = far[np.random.randint(len(far))]
    return np.exp2(a.ravel()).repeat(32)


def f64(x):
    return np.asarray(x).astype(np.float64)


def striped8(idx):
    return np.concatenate([x.reshape(-1, 16).T for x in idx]).astype(np.uint16)


def runs(offs, k):
    lists = np.stack([offs[16 * r : 16 * r + 16].T.reshape(-1) for r in range(8)]).astype(np.int64)
    return lists[np.arange(k) % 512 // 64]


def pack_weight(w):
    k, n = w.shape
    w = f64(np.asarray(w, np.float32).astype(ml_dtypes.bfloat16)).reshape(k // 32, 32, n)
    amax = np.abs(w).max(1)
    byte = np.clip(np.where(amax > 0, np.frexp(amax)[1] - 1 + 127 - 7, 1), 1, 254)
    scaled = (w * np.exp2(127.0 - byte)[:, None, :]).reshape(k, n).astype(np.float32)
    words = np.ascontiguousarray(scaled.reshape(k // 512, 128, 4, n).transpose(0, 1, 3, 2)).astype(ml_dtypes.float8_e4m3fn).view(np.uint8)
    return words, np.ascontiguousarray(byte.astype(np.uint8).reshape(k // 512, 16, n))


def unpack_weight(words, scales):
    g, p, n, _ = words.shape
    vals = np.ascontiguousarray(words).view(ml_dtypes.float8_e4m3fn).astype(np.float64) * np.repeat(np.exp2(scales.astype(np.float64) - 127.0), 8, axis=1)[..., None]
    return vals.transpose(0, 1, 3, 2).reshape(g * 512, n)


def relu(v):
    return np.maximum(v, 0.0)


K, T, S, N, H = 512, 2048, 512, 512, 512


def setup_inputs():
    n = np.random.standard_normal
    s = mx_kscale(K)[:, None]
    u = mx_kscale(H)
    packed_xT = pack_weight(n((K, T)) * s)
    return {
        "x_words": packed_xT[0],
        "x_scales": packed_xT[1],
        "w1": (n((K, H)) / np.sqrt(K) / s).astype(np.float32),
        "gn": (np.random.uniform(0.5, 1.5, (H, 1)) * u[:, None]).astype(np.float32),
        "w2": (n((H, N)) / np.sqrt(H) / u[:, None]).astype(np.float32),
        "offs": striped8(np.random.randint(0, T, (8, S))),
        "n1": striped8(np.stack([np.random.permutation(S) for _ in range(8)])),
        "n2": striped8(np.stack([np.random.permutation(S) for _ in range(8)])),
        "n3": striped8(np.stack([np.random.permutation(S) for _ in range(8)])),
        "n4": striped8(np.stack([np.random.permutation(S) for _ in range(8)])),
    }


def reference(x_words, x_scales, w1, gn, w2, offs, n1, n2, n3, n4):
    xq = unpack_weight(x_words, x_scales)[np.arange(K)[:, None], runs(offs, K)]
    y = mxq(f64(w1), 0, "e4m3").T @ xq
    z = f64(gn) * (y[np.arange(H)[:, None], runs(n1, H)] - (y[np.arange(H)[:, None], runs(n2, H)]))
    h = mxq(f64(w2), 0, "e4m3").T @ mxq(z, 0, "e4m3")
    return relu(h - (h[np.arange(N)[:, None], runs(n3, N)])) + 0.5 * (relu(h[np.arange(N)[:, None], runs(n4, N)] - h))

@@ -1,0 +1,184 @@
+from contextlib import ExitStack
+
+import concourse.mybir as mybir
+
+K, T, S, N, H = 512, 2048, 512, 512, 512
+FLOPS = 2 * K * H * S + 2 * H * N * S
+
+F32 = mybir.dt.float32
+BF16 = mybir.dt.bfloat16
+I32 = mybir.dt.int32
+U32 = mybir.dt.uint32
+U16 = mybir.dt.uint16
+U8 = mybir.dt.uint8
+FP8X4 = mybir.dt.float8_e4m3fn_x4
+ALU = mybir.AluOpType
+ACT = mybir.ActivationFunctionType
+
+P = 128
+PACK = 4
+LANES = 16
+Y_CHUNKS = ((0, 256), (256, 512))
+Z_CHUNKS = ((0, 256), (256, 384), (384, 512))
+
+
+def entries(offsets, a, b):
+    return offsets[:, a // LANES : b // LANES]
+
+
+def tile_picked_hashgaphinge_none_p_kernel(tc, x_words, x_scales, w1, gn, w2, offs, n1, n2, n3, n4, out):
+    nc = tc.nc
+    with ExitStack() as ctx:
+        keep = ctx.enter_context(tc.tile_pool(name="keep", bufs=1))
+        psum = ctx.enter_context(tc.psum_pool(name="psum", bufs=8))
+
+        lists = {}
+        for name in ("offs", "n1", "n2", "n3", "n4"):
+            lists[name] = keep.tile([P, S // LANES], U16, name="list_" + name)
+
+        scale_table = keep.tile([P, T], U8, name="scale_table", align_bytes=64)
+        word_table = keep.tile([P, T], U32, name="word_table", align_bytes=64)
+        w1_raw = keep.tile([P, PACK, H], F32, name="w1_raw", tag="stage", align_bytes=64)
+        gain = keep.tile([P, PACK], F32, name="gain")
+        x_scale_plane = keep.tile([P, S], U8, name="x_scale_plane", align_bytes=64)
+
+        nc.gpsimd.memset(scale_table[:].bitcast(I32), 0)
+        nc.scalar.dma_start(out=scale_table[0:P:8, :].bitcast(I32), in_=x_scales[0].bitcast(I32))
+        nc.gpsimd.memset(x_scale_plane[:].bitcast(I32), 0)
+
+        nc.sync.dma_start(lists["offs"][:], offs)
+        nc.sync.dma_start(out=w1_raw[:], in_=w1.rearrange("(p j) c -> p j c", j=PACK))
+        nc.sync.dma_start(lists["n2"][:], n2)
+        nc.sync.dma_start(lists["n1"][:], n1)
+        nc.sync.dma_start(out=gain[:], in_=gn.rearrange("(p t) o -> p (t o)", t=PACK))
+        nc.sync.dma_start(out=word_table[:].bitcast(I32), in_=x_words[0].rearrange("p n t -> p (n t)").bitcast(I32))
+        nc.sync.dma_start(lists["n3"][:], n3)
+        nc.sync.dma_start(lists["n4"][:], n4)
+
+        h_pos = [keep.tile([P, 2 * S], F32, name=f"h_pos{t}") for t in range(PACK)]
+        h_neg = [keep.tile([P, 2 * S], F32, name=f"h_neg{t}") for t in range(PACK)]
+        for t in range(PACK):
+            nc.gpsimd.memset(h_pos[t][:, S:], 0.0)
+            nc.gpsimd.memset(h_neg[t][:, S:], 0.0)
+
+        picked_scales = keep.tile([P, S], U8, name="picked_scales", align_bytes=64)
+        nc.vector.tensor_copy(picked_scales[:], scale_table[:].indirect(lists["offs"][:]))
+        for r in range(4):
+            nc.scalar.dma_start(out=x_scale_plane[r:P:32, :].bitcast(I32), in_=picked_scales[8 * r : P : 32, :].bitcast(I32))
+
+        def dealt(grouped, raw, m0, m1):
+            return (
+                grouped[:].rearrange("p (t m j) -> p m t j", t=PACK, j=PACK)[:, m0:m1],
+                raw[:].rearrange("p j (m t) -> p m t j", t=PACK)[:, m0:m1],
+            )
+
+        w1_grouped = keep.tile([P, PACK * H], BF16, name="w1_grouped", align_bytes=64)
+        w1_codes = keep.tile([P, H], U32, name="w1_codes", align_bytes=64)
+        w1_scales = keep.tile([P, H], U8, name="w1_scales", align_bytes=64)
+        dst, src = dealt(w1_grouped, w1_raw, 0, P)
+        nc.vector.tensor_copy(dst, src)
+        nc.vector.quantize_mx(out=w1_codes[:].bitcast(FP8X4), scales=w1_scales[:], in_=w1_grouped[:])
+
+        y = [keep.tile([P, S], F32, name=f"y{t}") for t in range(PACK)]
+        banks = {}
+        for c, (a, b) in enumerate(Y_CHUNKS):
+            picked = keep.tile([P, b - a], U32, name=f"picked_words{c}", align_bytes=64)
+            nc.vector.tensor_copy(picked[:], word_table[:].indirect(entries(lists["offs"], a, b)))
+            for t in range(PACK):
+                bank = psum.tile([P, b - a], F32, name="bank")
+                nc.tensor.matmul_mx(
+                    out=bank[:],
+                    lhsT=w1_codes[:, t * P : (t + 1) * P].bitcast(FP8X4),
+                    lhsT_scale=w1_scales[:, t * P : (t + 1) * P],
+                    rhs=picked[:].bitcast(FP8X4),
+                    rhs_scale=x_scale_plane[:, a:b],
+                    start=True,
+                    stop=True,
+                )
+                banks[c, t] = bank
+        for t in range(PACK):
+            for c, (a, b) in enumerate(Y_CHUNKS):
+                nc.scalar.activation(y[t][:, a:b], banks[c, t][:], ACT.Copy, scale=gain[:, t : t + 1])
+
+        w2_raw = keep.tile([P, PACK, N], F32, name="w2_raw", tag="stage", align_bytes=64)
+        nc.sync.dma_start(out=w2_raw[:], in_=w2.rearrange("(p j) c -> p j c", j=PACK))
+        w2_grouped = keep.tile([P, PACK * N], BF16, name="w2_grouped", align_bytes=64)
+        for m0 in range(0, P, 32):
+            dst, src = dealt(w2_grouped, w2_raw, m0, m0 + 32)
+            nc.scalar.copy(dst, src)
+        w2_scales = keep.tile([P, N], U8, name="w2_scales", align_bytes=64)
+        w2_codes_first = keep.tile([P, P], U32, name="w2_codes_first", align_bytes=64)
+        nc.vector.quantize_mx(out=w2_codes_first[:].bitcast(FP8X4), scales=w2_scales[:, :P], in_=w2_grouped[:, : PACK * P])
+
+        def interleave(engine_copy, z_grouped, z, a, b):
+            engine_copy(
+                z_grouped[:].rearrange("p (c i t) -> p c t i", i=4, t=PACK)[:, a // 4 : b // 4],
+                z[:].rearrange("p t (c i) -> p c t i", i=4)[:, a // 4 : b // 4],
+            )
+
+        h_banks = [psum.tile([P, S], F32, name="bank") for t in range(PACK)]
+        z_ops = []
+
+        def second_product(t, w2_codes, c):
+            a, b = Z_CHUNKS[c]
+            nc.tensor.matmul_mx(
+                out=h_banks[t][:, a:b],
+                lhsT=w2_codes.bitcast(FP8X4),
+                lhsT_scale=w2_scales[:, t * P : (t + 1) * P],
+                rhs=z_ops[c][0][:].bitcast(FP8X4),
+                rhs_scale=z_ops[c][1][:],
+                start=True,
+                stop=True,
+            )
+
+        def leave_bank(t, a, b):
+            nc.scalar.activation(h_pos[t][:, a:b], h_banks[t][:, a:b], ACT.Copy)
+            nc.scalar.activation(h_neg[t][:, a:b], h_banks[t][:, a:b], ACT.Copy, scale=-1.0)
+
+        second_tags = {(2, 0): "stage", (2, 2): "late"}
+        grouped_tags = {0: "stage", 1: "late", 2: "z_grouped_last"}
+        for c, (a, b) in enumerate(Z_CHUNKS):
+            width = b - a
+            z = keep.tile([P, PACK, width], F32, name=f"z{c}")
+            for pair in (0, 2):
+                second = keep.tile([P, 2, width], F32, name=f"second{c}_{pair}", tag=second_tags.get((c, pair), f"second{c}_{pair}"), align_bytes=64)
+                for e in (0, 1):
+                    nc.vector.tensor_copy(second[:, e, :], y[pair + e][:].indirect(entries(lists["n2"], a, b)))
+                for e in (0, 1):
+                    nc.vector.tensor_tensor(z[:, pair + e, :], y[pair + e][:].indirect(entries(lists["n1"], a, b)), second[:, e, :], ALU.subtract)
+            z_grouped = keep.tile([P, PACK * width], BF16, name=f"z_grouped{c}", tag=grouped_tags[c], align_bytes=64)
+            z_codes = keep.tile([P, width], U32, name=f"z_codes{c}", align_bytes=64)
+            z_scales = keep.tile([P, width], U8, name=f"z_scales{c}", align_bytes=64)
+            if c < len(Z_CHUNKS) - 1:
+                interleave(nc.scalar.copy, z_grouped, z, 0, width)
+            else:
+                interleave(nc.scalar.copy, z_grouped, z, 0, width // 2)
+                interleave(nc.vector.tensor_copy, z_grouped, z, width // 2, width)
+            nc.vector.quantize_mx(out=z_codes[:].bitcast(FP8X4), scales=z_scales[:], in_=z_grouped[:])
+            z_ops.append((z_codes, z_scales))
+            second_product(0, w2_codes_first[:], c)
+            leave_bank(0, a, b)
+
+        w2_codes_rest = keep.tile([P, N - P], U32, name="w2_codes_rest", tag="z_grouped_last", align_bytes=64)
+        nc.vector.quantize_mx(out=w2_codes_rest[:, :P].bitcast(FP8X4), scales=w2_scales[:, P : 2 * P], in_=w2_grouped[:, PACK * P : PACK * 2 * P])
+        nc.vector.quantize_mx(out=w2_codes_rest[:, P:].bitcast(FP8X4), scales=w2_scales[:, 2 * P :], in_=w2_grouped[:, PACK * 2 * P :])
+        for t in range(1, PACK):
+            for c in range(len(Z_CHUNKS)):
+                second_product(t, w2_codes_rest[:, (t - 1) * P : t * P], c)
+
+        out_rows = out.rearrange("(p t) j -> p t j", t=PACK)
+        for t in range(PACK):
+            if t > 0:
+                leave_bank(t, 0, S)
+            pieces = ((0, S),) if t < PACK - 1 else ((0, S // 2), (S // 2, S))
+            rise = keep.tile([P, S], F32, name=f"rise{t}")
+            half = keep.tile([P, S], F32, name=f"half{t}")
+            result = keep.tile([P, S], F32, name=f"result{t}")
+            nc.vector.tensor_tensor(rise[:], h_pos[t][:].indirect(lists["n4"][:]), h_neg[t][:, :S], ALU.add)
+            nc.scalar.activation(half[:], rise[:], ACT.Relu, scale=0.5)
+            drop = keep.tile([P, S], F32, name=f"drop{t}", tag="drop")
+            for a, b in pieces:
+                nc.vector.tensor_tensor(drop[:, a:b], h_neg[t][:].indirect(entries(lists["n3"], a, b)), h_pos[t][:, a:b], ALU.add)
+            for a, b in pieces:
+                nc.vector.scalar_tensor_tensor(result[:, a:b], drop[:, a:b], 0.0, half[:, a:b], ALU.max, ALU.add)
+                nc.sync.dma_start(out=out_rows[:, t, a:b], in_=result[:, a:b])

@@ -18,8 +18,8 @@ ACT = mybir.ActivationFunctionType
 P = 128
 PACK = 4
 LANES = 16
-Y_CHUNKS = ((0, 256), (256, 512))
-Z_CHUNKS = ((0, 256), (256, 384), (384, 512))
+HALF = S // 2
+HALVES = ((0, HALF), (HALF, S))
 
 
 def entries(offsets, a, b):
@@ -50,16 +50,8 @@ def tile_picked_hashgaphinge_none_p_kernel(tc, x_words, x_scales, w1, gn, w2, of
         nc.sync.dma_start(out=w1_raw[:], in_=w1.rearrange("(p j) c -> p j c", j=PACK))
         nc.sync.dma_start(lists["n2"][:], n2)
         nc.sync.dma_start(lists["n1"][:], n1)
-        nc.sync.dma_start(out=gain[:], in_=gn.rearrange("(p t) o -> p (t o)", t=PACK))
         nc.sync.dma_start(out=word_table[:].bitcast(I32), in_=x_words[0].rearrange("p n t -> p (n t)").bitcast(I32))
-        nc.sync.dma_start(lists["n3"][:], n3)
-        nc.sync.dma_start(lists["n4"][:], n4)
-
-        h_pos = [keep.tile([P, 2 * S], F32, name=f"h_pos{t}") for t in range(PACK)]
-        h_neg = [keep.tile([P, 2 * S], F32, name=f"h_neg{t}") for t in range(PACK)]
-        for t in range(PACK):
-            nc.gpsimd.memset(h_pos[t][:, S:], 0.0)
-            nc.gpsimd.memset(h_neg[t][:, S:], 0.0)
+        nc.gpsimd.dma_start(out=gain[:], in_=gn.rearrange("(p t) o -> p (t o)", t=PACK))
 
         picked_scales = keep.tile([P, S], U8, name="picked_scales", align_bytes=64)
         nc.vector.tensor_copy(picked_scales[:], scale_table[:].indirect(lists["offs"][:]))
@@ -80,28 +72,37 @@ def tile_picked_hashgaphinge_none_p_kernel(tc, x_words, x_scales, w1, gn, w2, of
         nc.vector.quantize_mx(out=w1_codes[:].bitcast(FP8X4), scales=w1_scales[:], in_=w1_grouped[:])
 
         y = [keep.tile([P, S], F32, name=f"y{t}") for t in range(PACK)]
-        banks = {}
-        for c, (a, b) in enumerate(Y_CHUNKS):
-            picked = keep.tile([P, b - a], U32, name=f"picked_words{c}", align_bytes=64)
-            nc.vector.tensor_copy(picked[:], word_table[:].indirect(entries(lists["offs"], a, b)))
-            for t in range(PACK):
-                bank = psum.tile([P, b - a], F32, name="bank")
-                nc.tensor.matmul_mx(
-                    out=bank[:],
-                    lhsT=w1_codes[:, t * P : (t + 1) * P].bitcast(FP8X4),
-                    lhsT_scale=w1_scales[:, t * P : (t + 1) * P],
-                    rhs=picked[:].bitcast(FP8X4),
-                    rhs_scale=x_scale_plane[:, a:b],
-                    start=True,
-                    stop=True,
-                )
-                banks[c, t] = bank
-        for t in range(PACK):
-            for c, (a, b) in enumerate(Y_CHUNKS):
-                nc.scalar.activation(y[t][:, a:b], banks[c, t][:], ACT.Copy, scale=gain[:, t : t + 1])
+        first_banks = [psum.tile([P, HALF], F32, name="bank") for c in range(2)]
+        y_banks = [None] + [psum.tile([P, S], F32, name="bank") for t in range(1, PACK)]
+        picked = keep.tile([P, S], U32, name="picked_words", align_bytes=64)
+
+        def first_product(bank, t, a, b):
+            nc.tensor.matmul_mx(
+                out=bank,
+                lhsT=w1_codes[:, t * P : (t + 1) * P].bitcast(FP8X4),
+                lhsT_scale=w1_scales[:, t * P : (t + 1) * P],
+                rhs=picked[:, a:b].bitcast(FP8X4),
+                rhs_scale=x_scale_plane[:, a:b],
+                start=True,
+                stop=True,
+            )
+
+        for c, (a, b) in enumerate(HALVES):
+            nc.vector.tensor_copy(picked[:, a:b], word_table[:].indirect(entries(lists["offs"], a, b)))
+            first_product(first_banks[c][:], 0, a, b)
+            first_product(y_banks[1][:, a:b], 1, a, b)
+        for t in (2, 3):
+            first_product(y_banks[t][:], t, 0, S)
+        for c, (a, b) in enumerate(HALVES):
+            nc.scalar.activation(y[0][:, a:b], first_banks[c][:], ACT.Copy, scale=gain[:, 0:1])
+        for t in range(1, PACK):
+            nc.scalar.activation(y[t][:], y_banks[t][:], ACT.Copy, scale=gain[:, t : t + 1])
+
 
         w2_raw = keep.tile([P, PACK, N], F32, name="w2_raw", tag="stage", align_bytes=64)
         nc.sync.dma_start(out=w2_raw[:], in_=w2.rearrange("(p j) c -> p j c", j=PACK))
+        nc.sync.dma_start(lists["n3"][:], n3)
+        nc.sync.dma_start(lists["n4"][:], n4)
         w2_grouped = keep.tile([P, PACK * N], BF16, name="w2_grouped", align_bytes=64)
         for m0 in range(0, P, 32):
             dst, src = dealt(w2_grouped, w2_raw, m0, m0 + 32)
@@ -112,15 +113,17 @@ def tile_picked_hashgaphinge_none_p_kernel(tc, x_words, x_scales, w1, gn, w2, of
 
         def interleave(engine_copy, z_grouped, z, a, b):
             engine_copy(
-                z_grouped[:].rearrange("p (c i t) -> p c t i", i=4, t=PACK)[:, a // 4 : b // 4],
-                z[:].rearrange("p t (c i) -> p c t i", i=4)[:, a // 4 : b // 4],
+                z_grouped.rearrange("p (c i t) -> p c t i", i=4, t=PACK)[:, a // 4 : b // 4],
+                z.rearrange("p (t c i) -> p c t i", i=4, t=PACK)[:, a // 4 : b // 4],
             )
 
         h_banks = [psum.tile([P, S], F32, name="bank") for t in range(PACK)]
+        h_window = [keep.tile([P, 2 * S], F32, name=f"h_window{t}") for t in range(PACK)]
+        h_plain = [keep.tile([P, S], F32, name=f"h_plain{t}") for t in range(PACK)]
         z_ops = []
 
         def second_product(t, w2_codes, c):
-            a, b = Z_CHUNKS[c]
+            a, b = HALVES[c]
             nc.tensor.matmul_mx(
                 out=h_banks[t][:, a:b],
                 lhsT=w2_codes.bitcast(FP8X4),
@@ -132,53 +135,51 @@ def tile_picked_hashgaphinge_none_p_kernel(tc, x_words, x_scales, w1, gn, w2, of
             )
 
         def leave_bank(t, a, b):
-            nc.scalar.activation(h_pos[t][:, a:b], h_banks[t][:, a:b], ACT.Copy)
-            nc.scalar.activation(h_neg[t][:, a:b], h_banks[t][:, a:b], ACT.Copy, scale=-1.0)
+            nc.scalar.activation(h_window[t][:, a:b], h_banks[t][:, a:b], ACT.Copy, scale=0.5)
+            nc.scalar.activation(h_plain[t][:, a:b], h_banks[t][:, a:b], ACT.Copy, scale=0.5)
 
-        second_tags = {(2, 0): "stage", (2, 2): "late"}
-        grouped_tags = {0: "stage", 1: "late", 2: "z_grouped_last"}
-        for c, (a, b) in enumerate(Z_CHUNKS):
-            width = b - a
-            z = keep.tile([P, PACK, width], F32, name=f"z{c}")
+        z = [keep.tile([P, PACK * HALF], F32, name=f"z{c}", tag=("z_first", "stage")[c], align_bytes=64) for c in range(2)]
+        z_grouped_last = keep.tile([P, PACK * HALF], BF16, name="z_grouped_last", tag="z_grouped_last", align_bytes=64)
+        z_grouped = [z[1][:, 2 * HALF :].bitcast(BF16), z_grouped_last[:]]
+        for c, (a, b) in enumerate(HALVES):
             for pair in (0, 2):
-                second = keep.tile([P, 2, width], F32, name=f"second{c}_{pair}", tag=second_tags.get((c, pair), f"second{c}_{pair}"), align_bytes=64)
-                for e in (0, 1):
-                    nc.vector.tensor_copy(second[:, e, :], y[pair + e][:].indirect(entries(lists["n2"], a, b)))
-                for e in (0, 1):
-                    nc.vector.tensor_tensor(z[:, pair + e, :], y[pair + e][:].indirect(entries(lists["n1"], a, b)), second[:, e, :], ALU.subtract)
-            z_grouped = keep.tile([P, PACK * width], BF16, name=f"z_grouped{c}", tag=grouped_tags[c], align_bytes=64)
-            z_codes = keep.tile([P, width], U32, name=f"z_codes{c}", align_bytes=64)
-            z_scales = keep.tile([P, width], U8, name=f"z_scales{c}", align_bytes=64)
-            if c < len(Z_CHUNKS) - 1:
-                interleave(nc.scalar.copy, z_grouped, z, 0, width)
+                for t in (pair, pair + 1):
+                    nc.vector.tensor_copy(h_window[t][:, S + a : S + b], y[t][:].indirect(entries(lists["n2"], a, b)))
+                for t in (pair, pair + 1):
+                    nc.vector.tensor_tensor(z[c][:, t * HALF : (t + 1) * HALF], y[t][:].indirect(entries(lists["n1"], a, b)), h_window[t][:, S + a : S + b], ALU.subtract)
+            z_codes = keep.tile([P, HALF], U32, name=f"z_codes{c}", align_bytes=64)
+            z_scales = keep.tile([P, HALF], U8, name=f"z_scales{c}", align_bytes=64)
+            if c == 0:
+                interleave(nc.scalar.copy, z_grouped[c], z[c][:], 0, HALF)
             else:
-                interleave(nc.scalar.copy, z_grouped, z, 0, width // 2)
-                interleave(nc.vector.tensor_copy, z_grouped, z, width // 2, width)
-            nc.vector.quantize_mx(out=z_codes[:].bitcast(FP8X4), scales=z_scales[:], in_=z_grouped[:])
+                interleave(nc.scalar.copy, z_grouped[c], z[c][:], 0, 96)
+                interleave(nc.vector.tensor_copy, z_grouped[c], z[c][:], 96, HALF)
+            nc.vector.quantize_mx(out=z_codes[:].bitcast(FP8X4), scales=z_scales[:], in_=z_grouped[c])
             z_ops.append((z_codes, z_scales))
             second_product(0, w2_codes_first[:], c)
             leave_bank(0, a, b)
+
 
         w2_codes_rest = keep.tile([P, N - P], U32, name="w2_codes_rest", tag="z_grouped_last", align_bytes=64)
         nc.vector.quantize_mx(out=w2_codes_rest[:, :P].bitcast(FP8X4), scales=w2_scales[:, P : 2 * P], in_=w2_grouped[:, PACK * P : PACK * 2 * P])
         nc.vector.quantize_mx(out=w2_codes_rest[:, P:].bitcast(FP8X4), scales=w2_scales[:, 2 * P :], in_=w2_grouped[:, PACK * 2 * P :])
         for t in range(1, PACK):
-            for c in range(len(Z_CHUNKS)):
+            for c in range(2):
                 second_product(t, w2_codes_rest[:, (t - 1) * P : t * P], c)
 
         out_rows = out.rearrange("(p t) j -> p t j", t=PACK)
         for t in range(PACK):
             if t > 0:
                 leave_bank(t, 0, S)
-            pieces = ((0, S),) if t < PACK - 1 else ((0, S // 2), (S // 2, S))
-            rise = keep.tile([P, S], F32, name=f"rise{t}")
-            half = keep.tile([P, S], F32, name=f"half{t}")
+            pieces = ((0, S),) if t < PACK - 1 else HALVES
+            drop = keep.tile([P, S], F32, name=f"drop{t}")
+            hinge = keep.tile([P, S], F32, name=f"hinge{t}")
             result = keep.tile([P, S], F32, name=f"result{t}")
-            nc.vector.tensor_tensor(rise[:], h_pos[t][:].indirect(lists["n4"][:]), h_neg[t][:, :S], ALU.add)
-            nc.scalar.activation(half[:], rise[:], ACT.Relu, scale=0.5)
-            drop = keep.tile([P, S], F32, name=f"drop{t}", tag="drop")
+            nc.vector.tensor_tensor(drop[:], h_window[t][:].indirect(lists["n3"][:]), h_plain[t][:], ALU.subtract)
+            nc.scalar.activation(hinge[:], drop[:], ACT.Relu, scale=-2.0)
+            rise = keep.tile([P, S], F32, name=f"rise{t}", tag="rise")
             for a, b in pieces:
-                nc.vector.tensor_tensor(drop[:, a:b], h_neg[t][:].indirect(entries(lists["n3"], a, b)), h_pos[t][:, a:b], ALU.add)
+                nc.vector.tensor_tensor(rise[:, a:b], h_window[t][:].indirect(entries(lists["n4"], a, b)), h_plain[t][:, a:b], ALU.subtract)
             for a, b in pieces:
-                nc.vector.scalar_tensor_tensor(result[:, a:b], drop[:, a:b], 0.0, half[:, a:b], ALU.max, ALU.add)
+                nc.vector.scalar_tensor_tensor(result[:, a:b], rise[:, a:b], 0.0, hinge[:, a:b], ALU.max, ALU.add)
                 nc.sync.dma_start(out=out_rows[:, t, a:b], in_=result[:, a:b])

@@ -1,6 +1,7 @@
 from contextlib import ExitStack
 
 import concourse.mybir as mybir
+from concourse.masks import make_identity
 
 K, T, S, N, H = 512, 2048, 512, 512, 512
 FLOPS = 2 * K * H * S + 2 * H * N * S
@@ -43,20 +44,26 @@ def tile_picked_hashgaphinge_none_p_kernel(tc, x_words, x_scales, w1, gn, w2, of
         x_scale_plane = keep.tile([P, S], U8, name="x_scale_plane", align_bytes=64)
 
         nc.gpsimd.memset(scale_table[:].bitcast(I32), 0)
-        nc.scalar.dma_start(out=scale_table[0:P:8, :].bitcast(I32), in_=x_scales[0].bitcast(I32))
         nc.gpsimd.memset(x_scale_plane[:].bitcast(I32), 0)
 
         nc.sync.dma_start(lists["offs"][:], offs)
-        nc.sync.dma_start(out=w1_raw[:], in_=w1.rearrange("(p j) c -> p j c", j=PACK))
         nc.sync.dma_start(lists["n2"][:], n2)
         nc.sync.dma_start(lists["n1"][:], n1)
+        w1_rows = w1.rearrange("(p j) c -> p j c", j=PACK)
+        nc.sync.dma_start(out=w1_raw[:, 0, :], in_=w1_rows[:, 0, :])
+        nc.sync.dma_start(out=scale_table[0:P:8, :].bitcast(I32), in_=x_scales[0].bitcast(I32))
+        nc.sync.dma_start(out=w1_raw[:, 1:, :], in_=w1_rows[:, 1:, :])
+        nc.sync.dma_start(out=gain[:], in_=gn.rearrange("(p t) o -> p (t o)", t=PACK))
         nc.sync.dma_start(out=word_table[:].bitcast(I32), in_=x_words[0].rearrange("p n t -> p (n t)").bitcast(I32))
-        nc.gpsimd.dma_start(out=gain[:], in_=gn.rearrange("(p t) o -> p (t o)", t=PACK))
+        nc.sync.dma_start(lists["n3"][:], n3)
+        nc.sync.dma_start(lists["n4"][:], n4)
+        identity = keep.tile([P, P], F32, name="identity")
+        make_identity(nc, identity[:])
 
         picked_scales = keep.tile([P, S], U8, name="picked_scales", align_bytes=64)
         nc.vector.tensor_copy(picked_scales[:], scale_table[:].indirect(lists["offs"][:]))
         for r in range(4):
-            nc.scalar.dma_start(out=x_scale_plane[r:P:32, :].bitcast(I32), in_=picked_scales[8 * r : P : 32, :].bitcast(I32))
+            nc.sync.dma_start(out=x_scale_plane[r:P:32, :].bitcast(I32), in_=picked_scales[8 * r : P : 32, :].bitcast(I32))
 
         def dealt(grouped, raw, m0, m1):
             return (
@@ -101,15 +108,13 @@ def tile_picked_hashgaphinge_none_p_kernel(tc, x_words, x_scales, w1, gn, w2, of
 
         w2_raw = keep.tile([P, PACK, N], F32, name="w2_raw", tag="stage", align_bytes=64)
         nc.sync.dma_start(out=w2_raw[:], in_=w2.rearrange("(p j) c -> p j c", j=PACK))
-        nc.sync.dma_start(lists["n3"][:], n3)
-        nc.sync.dma_start(lists["n4"][:], n4)
         w2_grouped = keep.tile([P, PACK * N], BF16, name="w2_grouped", align_bytes=64)
         for m0 in range(0, P, 32):
             dst, src = dealt(w2_grouped, w2_raw, m0, m0 + 32)
             nc.scalar.copy(dst, src)
         w2_scales = keep.tile([P, N], U8, name="w2_scales", align_bytes=64)
-        w2_codes_first = keep.tile([P, P], U32, name="w2_codes_first", align_bytes=64)
-        nc.vector.quantize_mx(out=w2_codes_first[:].bitcast(FP8X4), scales=w2_scales[:, :P], in_=w2_grouped[:, : PACK * P])
+        w2_codes_first = keep.tile([P, 2 * P], U32, name="w2_codes_first", align_bytes=64)
+        nc.vector.quantize_mx(out=w2_codes_first[:].bitcast(FP8X4), scales=w2_scales[:, : 2 * P], in_=w2_grouped[:, : PACK * 2 * P])
 
         def interleave(engine_copy, z_grouped, z, a, b):
             engine_copy(
@@ -117,19 +122,21 @@ def tile_picked_hashgaphinge_none_p_kernel(tc, x_words, x_scales, w1, gn, w2, of
                 z.rearrange("p (t c i) -> p c t i", i=4, t=PACK)[:, a // 4 : b // 4],
             )
 
+        z_parts = ((0, HALF), (HALF + P, S), (HALF, HALF + P))
+        h0_banks = [psum.tile([P, b - a], F32, name="bank") for a, b in z_parts[1:]]
         h_banks = [psum.tile([P, S], F32, name="bank") for t in range(PACK)]
         h_window = [keep.tile([P, 2 * S], F32, name=f"h_window{t}") for t in range(PACK)]
         h_plain = [keep.tile([P, S], F32, name=f"h_plain{t}") for t in range(PACK)]
-        z_ops = []
+        z_codes = keep.tile([P, S], U32, name="z_codes", align_bytes=64)
+        z_scales = keep.tile([P, S], U8, name="z_scales", align_bytes=64)
 
-        def second_product(t, w2_codes, c):
-            a, b = HALVES[c]
+        def second_product(bank, t, w2_codes, a, b):
             nc.tensor.matmul_mx(
-                out=h_banks[t][:, a:b],
+                out=bank,
                 lhsT=w2_codes.bitcast(FP8X4),
                 lhsT_scale=w2_scales[:, t * P : (t + 1) * P],
-                rhs=z_ops[c][0][:].bitcast(FP8X4),
-                rhs_scale=z_ops[c][1][:],
+                rhs=z_codes[:, a:b].bitcast(FP8X4),
+                rhs_scale=z_scales[:, a:b],
                 start=True,
                 stop=True,
             )
@@ -147,39 +154,61 @@ def tile_picked_hashgaphinge_none_p_kernel(tc, x_words, x_scales, w1, gn, w2, of
                     nc.vector.tensor_copy(h_window[t][:, S + a : S + b], y[t][:].indirect(entries(lists["n2"], a, b)))
                 for t in (pair, pair + 1):
                     nc.vector.tensor_tensor(z[c][:, t * HALF : (t + 1) * HALF], y[t][:].indirect(entries(lists["n1"], a, b)), h_window[t][:, S + a : S + b], ALU.subtract)
-            z_codes = keep.tile([P, HALF], U32, name=f"z_codes{c}", align_bytes=64)
-            z_scales = keep.tile([P, HALF], U8, name=f"z_scales{c}", align_bytes=64)
             if c == 0:
-                interleave(nc.scalar.copy, z_grouped[c], z[c][:], 0, HALF)
-            else:
-                interleave(nc.scalar.copy, z_grouped[c], z[c][:], 0, 96)
-                interleave(nc.vector.tensor_copy, z_grouped[c], z[c][:], 96, HALF)
-            nc.vector.quantize_mx(out=z_codes[:].bitcast(FP8X4), scales=z_scales[:], in_=z_grouped[c])
-            z_ops.append((z_codes, z_scales))
-            second_product(0, w2_codes_first[:], c)
-            leave_bank(0, a, b)
+                interleave(nc.scalar.copy, z_grouped[0], z[0][:], 0, HALF)
+                nc.vector.quantize_mx(out=z_codes[:, :HALF].bitcast(FP8X4), scales=z_scales[:, :HALF], in_=z_grouped[0])
+                second_product(h_banks[0][:, :HALF], 0, w2_codes_first[:, :P], 0, HALF)
+                second_product(h_banks[1][:, :HALF], 1, w2_codes_first[:, P:], 0, HALF)
+                leave_bank(0, 0, HALF)
+        interleave(nc.scalar.copy, z_grouped[1], z[1][:], 0, P)
+        interleave(nc.vector.tensor_copy, z_grouped[1], z[1][:], P, HALF)
+        for bank, (a, b) in zip(h0_banks, z_parts[1:]):
+            nc.vector.quantize_mx(out=z_codes[:, a:b].bitcast(FP8X4), scales=z_scales[:, a:b], in_=z_grouped[1][:, PACK * (a - HALF) : PACK * (b - HALF)])
+            second_product(bank[:], 0, w2_codes_first[:, :P], a, b)
+        second_product(h_banks[1][:, HALF:], 1, w2_codes_first[:, P:], HALF, S)
+        a, b = z_parts[1]
+        nc.vector.tensor_scalar_mul(h_window[0][:, a:b], h0_banks[0][:], 0.5)
+        nc.vector.tensor_scalar_mul(h_plain[0][:, a:b], h0_banks[0][:], 0.5)
+        a, b = z_parts[2]
+        nc.scalar.activation(h_window[0][:, a:b], h0_banks[1][:], ACT.Copy, scale=0.5)
+        nc.scalar.activation(h_plain[0][:, a:b], h0_banks[1][:], ACT.Copy, scale=0.5)
 
-
-        w2_codes_rest = keep.tile([P, N - P], U32, name="w2_codes_rest", tag="z_grouped_last", align_bytes=64)
-        nc.vector.quantize_mx(out=w2_codes_rest[:, :P].bitcast(FP8X4), scales=w2_scales[:, P : 2 * P], in_=w2_grouped[:, PACK * P : PACK * 2 * P])
-        nc.vector.quantize_mx(out=w2_codes_rest[:, P:].bitcast(FP8X4), scales=w2_scales[:, 2 * P :], in_=w2_grouped[:, PACK * 2 * P :])
-        for t in range(1, PACK):
-            for c in range(2):
-                second_product(t, w2_codes_rest[:, (t - 1) * P : t * P], c)
+        w2_codes_rest = keep.tile([P, 2 * P], U32, name="w2_codes_rest", tag="z_grouped_last", align_bytes=64)
+        nc.vector.quantize_mx(out=w2_codes_rest[:].bitcast(FP8X4), scales=w2_scales[:, 2 * P :], in_=w2_grouped[:, PACK * 2 * P :])
+        for t in (2, 3):
+            second_product(h_banks[t][:], t, w2_codes_rest[:, (t - 2) * P : (t - 1) * P], 0, S)
 
         out_rows = out.rearrange("(p t) j -> p t j", t=PACK)
+        blocks = [slice(q * P, (q + 1) * P) for q in range(S // P)]
+        leave_bank(1, 0, S)
+        for t in (2, 3):
+            nc.scalar.activation(h_window[t][:, :S], h_banks[t][:], ACT.Copy, scale=0.5)
+            nc.sync.dma_start(out=h_plain[t][:], in_=h_window[t][:, :S])
         for t in range(PACK):
-            if t > 0:
-                leave_bank(t, 0, S)
             pieces = ((0, S),) if t < PACK - 1 else HALVES
             drop = keep.tile([P, S], F32, name=f"drop{t}")
-            hinge = keep.tile([P, S], F32, name=f"hinge{t}")
+            hinge = keep.tile([P, S], F32, name=f"hinge{t}", tag=f"lifted{t - 2}" if t >= 2 else f"hinge{t}")
             result = keep.tile([P, S], F32, name=f"result{t}")
             nc.vector.tensor_tensor(drop[:], h_window[t][:].indirect(lists["n3"][:]), h_plain[t][:], ALU.subtract)
             nc.scalar.activation(hinge[:], drop[:], ACT.Relu, scale=-2.0)
-            rise = keep.tile([P, S], F32, name=f"rise{t}", tag="rise")
+            rise = keep.tile([P, S], F32, name=f"rise{t}", tag="rise" if t >= 2 else f"rise{t}")
             for a, b in pieces:
                 nc.vector.tensor_tensor(rise[:, a:b], h_window[t][:].indirect(entries(lists["n4"], a, b)), h_plain[t][:, a:b], ALU.subtract)
-            for a, b in pieces:
-                nc.vector.scalar_tensor_tensor(result[:, a:b], rise[:, a:b], 0.0, hinge[:, a:b], ALU.max, ALU.add)
-                nc.sync.dma_start(out=out_rows[:, t, a:b], in_=result[:, a:b])
+            if t < 2:
+                lifted = keep.tile([P, S], F32, name=f"lifted{t}", tag=f"lifted{t}")
+                turned = keep.tile([P, S], F32, name=f"turned{t}")
+                nc.scalar.activation(lifted[:], rise[:], ACT.Relu)
+                summed = psum.tile([P, S], F32, name="bank")
+                for block in blocks:
+                    nc.tensor.matmul(summed[:, block], hinge[:, block], identity[:], start=True, stop=False, is_transpose=True)
+                    nc.tensor.matmul(summed[:, block], lifted[:, block], identity[:], start=False, stop=True, is_transpose=True)
+                nc.scalar.copy(turned[:], summed[:])
+                back = psum.tile([P, S], F32, name="bank")
+                for block in blocks:
+                    nc.tensor.transpose(back[:, block], turned[:, block], identity[:])
+                nc.scalar.copy(result[:], back[:])
+                nc.scalar.dma_start(out=out_rows[:, t, :], in_=result[:])
+            else:
+                for a, b in pieces:
+                    nc.vector.scalar_tensor_tensor(result[:, a:b], rise[:, a:b], 0.0, hinge[:, a:b], ALU.max, ALU.add)
+                    nc.sync.dma_start(out=out_rows[:, t, a:b], in_=result[:, a:b])

@@ -48,13 +48,13 @@ def tile_picked_hashgaphinge_none_p_kernel(tc, x_words, x_scales, w1, gn, w2, of
 
         nc.sync.dma_start(lists["offs"][:], offs)
         nc.sync.dma_start(lists["n2"][:], n2)
-        nc.sync.dma_start(lists["n1"][:], n1)
         w1_rows = w1.rearrange("(p j) c -> p j c", j=PACK)
         nc.sync.dma_start(out=w1_raw[:, 0, :], in_=w1_rows[:, 0, :])
         nc.sync.dma_start(out=scale_table[0:P:8, :].bitcast(I32), in_=x_scales[0].bitcast(I32))
         nc.sync.dma_start(out=w1_raw[:, 1:, :], in_=w1_rows[:, 1:, :])
         nc.sync.dma_start(out=gain[:], in_=gn.rearrange("(p t) o -> p (t o)", t=PACK))
         nc.sync.dma_start(out=word_table[:].bitcast(I32), in_=x_words[0].rearrange("p n t -> p (n t)").bitcast(I32))
+        nc.sync.dma_start(lists["n1"][:], n1)
         nc.sync.dma_start(lists["n3"][:], n3)
         nc.sync.dma_start(lists["n4"][:], n4)
         identity = keep.tile([P, P], F32, name="identity")
@@ -181,10 +181,10 @@ def tile_picked_hashgaphinge_none_p_kernel(tc, x_words, x_scales, w1, gn, w2, of
         out_rows = out.rearrange("(p t) j -> p t j", t=PACK)
         blocks = [slice(q * P, (q + 1) * P) for q in range(S // P)]
         leave_bank(1, 0, S)
-        for t in (2, 3):
-            nc.scalar.activation(h_window[t][:, :S], h_banks[t][:], ACT.Copy, scale=0.5)
-            nc.sync.dma_start(out=h_plain[t][:], in_=h_window[t][:, :S])
         for t in range(PACK):
+            if t < 2:
+                nc.scalar.activation(h_window[t + 2][:, :S], h_banks[t + 2][:], ACT.Copy, scale=0.5)
+                nc.sync.dma_start(out=h_plain[t + 2][:], in_=h_window[t + 2][:, :S])
             pieces = ((0, S),) if t < PACK - 1 else HALVES
             drop = keep.tile([P, S], F32, name=f"drop{t}")
             hinge = keep.tile([P, S], F32, name=f"hinge{t}", tag=f"lifted{t - 2}" if t >= 2 else f"hinge{t}")
@@ -199,9 +199,10 @@ def tile_picked_hashgaphinge_none_p_kernel(tc, x_words, x_scales, w1, gn, w2, of
                 turned = keep.tile([P, S], F32, name=f"turned{t}")
                 nc.scalar.activation(lifted[:], rise[:], ACT.Relu)
                 summed = psum.tile([P, S], F32, name="bank")
-                for block in blocks:
-                    nc.tensor.matmul(summed[:, block], hinge[:, block], identity[:], start=True, stop=False, is_transpose=True)
-                    nc.tensor.matmul(summed[:, block], lifted[:, block], identity[:], start=False, stop=True, is_transpose=True)
+                for q, block in enumerate(blocks):
+                    nc.tensor.matmul(summed[:, block], hinge[:, block], identity[:], start=(q == 0), stop=False, is_transpose=True)
+                for q, block in enumerate(blocks):
+                    nc.tensor.matmul(summed[:, block], lifted[:, block], identity[:], start=False, stop=(q == len(blocks) - 1), is_transpose=True)
                 nc.scalar.copy(turned[:], summed[:])
                 back = psum.tile([P, S], F32, name="bank")
                 for block in blocks:

from contextlib import ExitStack

import concourse.mybir as mybir
from concourse.masks import make_identity

K, T, S, N, H = 512, 2048, 512, 512, 512
FLOPS = 2 * K * H * S + 2 * H * N * S

F32 = mybir.dt.float32
BF16 = mybir.dt.bfloat16
I32 = mybir.dt.int32
U32 = mybir.dt.uint32
U16 = mybir.dt.uint16
U8 = mybir.dt.uint8
FP8X4 = mybir.dt.float8_e4m3fn_x4
ALU = mybir.AluOpType
ACT = mybir.ActivationFunctionType

P = 128
PACK = 4
LANES = 16
HALF = S // 2
HALVES = ((0, HALF), (HALF, S))


def entries(offsets, a, b):
    return offsets[:, a // LANES : b // LANES]


def tile_picked_hashgaphinge_none_p_kernel(tc, x_words, x_scales, w1, gn, w2, offs, n1, n2, n3, n4, out):
    nc = tc.nc
    with ExitStack() as ctx:
        keep = ctx.enter_context(tc.tile_pool(name="keep", bufs=1))
        psum = ctx.enter_context(tc.psum_pool(name="psum", bufs=8))

        lists = {}
        for name in ("offs", "n1", "n2", "n3", "n4"):
            lists[name] = keep.tile([P, S // LANES], U16, name="list_" + name)

        scale_table = keep.tile([P, T], U8, name="scale_table", align_bytes=64)
        word_table = keep.tile([P, T], U32, name="word_table", align_bytes=64)
        w1_raw = keep.tile([P, PACK, H], F32, name="w1_raw", tag="stage", align_bytes=64)
        gain = keep.tile([P, PACK], F32, name="gain")
        x_scale_plane = keep.tile([P, S], U8, name="x_scale_plane", align_bytes=64)

        nc.gpsimd.memset(scale_table[:].bitcast(I32), 0)
        nc.gpsimd.memset(x_scale_plane[:].bitcast(I32), 0)

        nc.sync.dma_start(lists["offs"][:], offs)
        nc.sync.dma_start(lists["n2"][:], n2)
        w1_rows = w1.rearrange("(p j) c -> p j c", j=PACK)
        nc.sync.dma_start(out=w1_raw[:, 0, :], in_=w1_rows[:, 0, :])
        nc.sync.dma_start(out=scale_table[0:P:8, :].bitcast(I32), in_=x_scales[0].bitcast(I32))
        nc.sync.dma_start(out=w1_raw[:, 1:, :], in_=w1_rows[:, 1:, :])
        nc.sync.dma_start(out=gain[:], in_=gn.rearrange("(p t) o -> p (t o)", t=PACK))
        nc.sync.dma_start(out=word_table[:].bitcast(I32), in_=x_words[0].rearrange("p n t -> p (n t)").bitcast(I32))
        nc.sync.dma_start(lists["n1"][:], n1)
        nc.sync.dma_start(lists["n3"][:], n3)
        nc.sync.dma_start(lists["n4"][:], n4)
        identity = keep.tile([P, P], F32, name="identity")
        make_identity(nc, identity[:])

        picked_scales = keep.tile([P, S], U8, name="picked_scales", align_bytes=64)
        nc.vector.tensor_copy(picked_scales[:], scale_table[:].indirect(lists["offs"][:]))
        for r in range(4):
            nc.sync.dma_start(out=x_scale_plane[r:P:32, :].bitcast(I32), in_=picked_scales[8 * r : P : 32, :].bitcast(I32))

        def dealt(grouped, raw, m0, m1):
            return (
                grouped[:].rearrange("p (t m j) -> p m t j", t=PACK, j=PACK)[:, m0:m1],
                raw[:].rearrange("p j (m t) -> p m t j", t=PACK)[:, m0:m1],
            )

        w1_grouped = keep.tile([P, PACK * H], BF16, name="w1_grouped", align_bytes=64)
        w1_codes = keep.tile([P, H], U32, name="w1_codes", align_bytes=64)
        w1_scales = keep.tile([P, H], U8, name="w1_scales", align_bytes=64)
        dst, src = dealt(w1_grouped, w1_raw, 0, P)
        nc.vector.tensor_copy(dst, src)
        nc.vector.quantize_mx(out=w1_codes[:].bitcast(FP8X4), scales=w1_scales[:], in_=w1_grouped[:])

        y = [keep.tile([P, S], F32, name=f"y{t}") for t in range(PACK)]
        first_banks = [psum.tile([P, HALF], F32, name="bank") for c in range(2)]
        y_banks = [None] + [psum.tile([P, S], F32, name="bank") for t in range(1, PACK)]
        picked = keep.tile([P, S], U32, name="picked_words", align_bytes=64)

        def first_product(bank, t, a, b):
            nc.tensor.matmul_mx(
                out=bank,
                lhsT=w1_codes[:, t * P : (t + 1) * P].bitcast(FP8X4),
                lhsT_scale=w1_scales[:, t * P : (t + 1) * P],
                rhs=picked[:, a:b].bitcast(FP8X4),
                rhs_scale=x_scale_plane[:, a:b],
                start=True,
                stop=True,
            )

        for c, (a, b) in enumerate(HALVES):
            nc.vector.tensor_copy(picked[:, a:b], word_table[:].indirect(entries(lists["offs"], a, b)))
            first_product(first_banks[c][:], 0, a, b)
            first_product(y_banks[1][:, a:b], 1, a, b)
        for t in (2, 3):
            first_product(y_banks[t][:], t, 0, S)
        for c, (a, b) in enumerate(HALVES):
            nc.scalar.activation(y[0][:, a:b], first_banks[c][:], ACT.Copy, scale=gain[:, 0:1])
        for t in range(1, PACK):
            nc.scalar.activation(y[t][:], y_banks[t][:], ACT.Copy, scale=gain[:, t : t + 1])


        w2_raw = keep.tile([P, PACK, N], F32, name="w2_raw", tag="stage", align_bytes=64)
        nc.sync.dma_start(out=w2_raw[:], in_=w2.rearrange("(p j) c -> p j c", j=PACK))
        w2_grouped = keep.tile([P, PACK * N], BF16, name="w2_grouped", align_bytes=64)
        for m0 in range(0, P, 32):
            dst, src = dealt(w2_grouped, w2_raw, m0, m0 + 32)
            nc.scalar.copy(dst, src)
        w2_scales = keep.tile([P, N], U8, name="w2_scales", align_bytes=64)
        w2_codes_first = keep.tile([P, 2 * P], U32, name="w2_codes_first", align_bytes=64)
        nc.vector.quantize_mx(out=w2_codes_first[:].bitcast(FP8X4), scales=w2_scales[:, : 2 * P], in_=w2_grouped[:, : PACK * 2 * P])

        def interleave(engine_copy, z_grouped, z, a, b):
            engine_copy(
                z_grouped.rearrange("p (c i t) -> p c t i", i=4, t=PACK)[:, a // 4 : b // 4],
                z.rearrange("p (t c i) -> p c t i", i=4, t=PACK)[:, a // 4 : b // 4],
            )

        z_parts = ((0, HALF), (HALF + P, S), (HALF, HALF + P))
        h0_banks = [psum.tile([P, b - a], F32, name="bank") for a, b in z_parts[1:]]
        h_banks = [psum.tile([P, S], F32, name="bank") for t in range(PACK)]
        h_window = [keep.tile([P, 2 * S], F32, name=f"h_window{t}") for t in range(PACK)]
        h_plain = [keep.tile([P, S], F32, name=f"h_plain{t}") for t in range(PACK)]
        z_codes = keep.tile([P, S], U32, name="z_codes", align_bytes=64)
        z_scales = keep.tile([P, S], U8, name="z_scales", align_bytes=64)

        def second_product(bank, t, w2_codes, a, b):
            nc.tensor.matmul_mx(
                out=bank,
                lhsT=w2_codes.bitcast(FP8X4),
                lhsT_scale=w2_scales[:, t * P : (t + 1) * P],
                rhs=z_codes[:, a:b].bitcast(FP8X4),
                rhs_scale=z_scales[:, a:b],
                start=True,
                stop=True,
            )

        def leave_bank(t, a, b):
            nc.scalar.activation(h_window[t][:, a:b], h_banks[t][:, a:b], ACT.Copy, scale=0.5)
            nc.scalar.activation(h_plain[t][:, a:b], h_banks[t][:, a:b], ACT.Copy, scale=0.5)

        z = [keep.tile([P, PACK * HALF], F32, name=f"z{c}", tag=("z_first", "stage")[c], align_bytes=64) for c in range(2)]
        z_grouped_last = keep.tile([P, PACK * HALF], BF16, name="z_grouped_last", tag="z_grouped_last", align_bytes=64)
        z_grouped = [z[1][:, 2 * HALF :].bitcast(BF16), z_grouped_last[:]]
        for c, (a, b) in enumerate(HALVES):
            for pair in (0, 2):
                for t in (pair, pair + 1):
                    nc.vector.tensor_copy(h_window[t][:, S + a : S + b], y[t][:].indirect(entries(lists["n2"], a, b)))
                for t in (pair, pair + 1):
                    nc.vector.tensor_tensor(z[c][:, t * HALF : (t + 1) * HALF], y[t][:].indirect(entries(lists["n1"], a, b)), h_window[t][:, S + a : S + b], ALU.subtract)
            if c == 0:
                interleave(nc.scalar.copy, z_grouped[0], z[0][:], 0, HALF)
                nc.vector.quantize_mx(out=z_codes[:, :HALF].bitcast(FP8X4), scales=z_scales[:, :HALF], in_=z_grouped[0])
                second_product(h_banks[0][:, :HALF], 0, w2_codes_first[:, :P], 0, HALF)
                second_product(h_banks[1][:, :HALF], 1, w2_codes_first[:, P:], 0, HALF)
                leave_bank(0, 0, HALF)
        interleave(nc.scalar.copy, z_grouped[1], z[1][:], 0, P)
        interleave(nc.vector.tensor_copy, z_grouped[1], z[1][:], P, HALF)
        for bank, (a, b) in zip(h0_banks, z_parts[1:]):
            nc.vector.quantize_mx(out=z_codes[:, a:b].bitcast(FP8X4), scales=z_scales[:, a:b], in_=z_grouped[1][:, PACK * (a - HALF) : PACK * (b - HALF)])
            second_product(bank[:], 0, w2_codes_first[:, :P], a, b)
        second_product(h_banks[1][:, HALF:], 1, w2_codes_first[:, P:], HALF, S)
        a, b = z_parts[1]
        nc.vector.tensor_scalar_mul(h_window[0][:, a:b], h0_banks[0][:], 0.5)
        nc.vector.tensor_scalar_mul(h_plain[0][:, a:b], h0_banks[0][:], 0.5)
        a, b = z_parts[2]
        nc.scalar.activation(h_window[0][:, a:b], h0_banks[1][:], ACT.Copy, scale=0.5)
        nc.scalar.activation(h_plain[0][:, a:b], h0_banks[1][:], ACT.Copy, scale=0.5)

        w2_codes_rest = keep.tile([P, 2 * P], U32, name="w2_codes_rest", tag="z_grouped_last", align_bytes=64)
        nc.vector.quantize_mx(out=w2_codes_rest[:].bitcast(FP8X4), scales=w2_scales[:, 2 * P :], in_=w2_grouped[:, PACK * 2 * P :])
        for t in (2, 3):
            second_product(h_banks[t][:], t, w2_codes_rest[:, (t - 2) * P : (t - 1) * P], 0, S)

        out_rows = out.rearrange("(p t) j -> p t j", t=PACK)
        blocks = [slice(q * P, (q + 1) * P) for q in range(S // P)]
        leave_bank(1, 0, S)
        for t in range(PACK):
            if t < 2:
                nc.scalar.activation(h_window[t + 2][:, :S], h_banks[t + 2][:], ACT.Copy, scale=0.5)
                nc.sync.dma_start(out=h_plain[t + 2][:], in_=h_window[t + 2][:, :S])
            pieces = ((0, S),) if t < PACK - 1 else HALVES
            drop = keep.tile([P, S], F32, name=f"drop{t}")
            hinge = keep.tile([P, S], F32, name=f"hinge{t}", tag=f"lifted{t - 2}" if t >= 2 else f"hinge{t}")
            result = keep.tile([P, S], F32, name=f"result{t}")
            nc.vector.tensor_tensor(drop[:], h_window[t][:].indirect(lists["n3"][:]), h_plain[t][:], ALU.subtract)
            nc.scalar.activation(hinge[:], drop[:], ACT.Relu, scale=-2.0)
            rise = keep.tile([P, S], F32, name=f"rise{t}", tag="rise" if t >= 2 else f"rise{t}")
            for a, b in pieces:
                nc.vector.tensor_tensor(rise[:, a:b], h_window[t][:].indirect(entries(lists["n4"], a, b)), h_plain[t][:, a:b], ALU.subtract)
            if t < 2:
                lifted = keep.tile([P, S], F32, name=f"lifted{t}", tag=f"lifted{t}")
                turned = keep.tile([P, S], F32, name=f"turned{t}")
                nc.scalar.activation(lifted[:], rise[:], ACT.Relu)
                summed = psum.tile([P, S], F32, name="bank")
                for q, block in enumerate(blocks):
                    nc.tensor.matmul(summed[:, block], hinge[:, block], identity[:], start=(q == 0), stop=False, is_transpose=True)
                for q, block in enumerate(blocks):
                    nc.tensor.matmul(summed[:, block], lifted[:, block], identity[:], start=False, stop=(q == len(blocks) - 1), is_transpose=True)
                nc.scalar.copy(turned[:], summed[:])
                back = psum.tile([P, S], F32, name="bank")
                for block in blocks:
                    nc.tensor.transpose(back[:, block], turned[:, block], identity[:])
                nc.scalar.copy(result[:], back[:])
                nc.scalar.dma_start(out=out_rows[:, t, :], in_=result[:])
            else:
                for a, b in pieces:
                    nc.vector.scalar_tensor_tensor(result[:, a:b], rise[:, a:b], 0.0, hinge[:, a:b], ALU.max, ALU.add)
                    nc.sync.dma_start(out=out_rows[:, t, a:b], in_=result[:, a:b])
